import numpy as np
import ml_dtypes

BF16 = ml_dtypes.bfloat16


def bf(x):
    return np.asarray(x, np.float32).astype(BF16)


def f32(x):
    return np.asarray(x, np.float32)


def f64(x):
    return np.asarray(x).astype(np.float64)


def striped(idx):
    return np.tile(idx.reshape(-1, 16).T, (8, 1))


S, K, M, N = 1024, 256, 128, 1024


def setup_inputs():
    return {"table": bf(np.random.standard_normal((K, S))), "w": bf(np.random.standard_normal((K, M)) / np.sqrt(K)), "b": f32(0.5 * np.random.standard_normal((M, 1))), "offs": striped(np.random.permutation(np.tile(np.arange(S), 2))[:N])}


def reference(table, w, b, offs):
    idx = offs[:16].T.reshape(-1)
    x = f64(table)[:, idx]
    y = f64(w).T @ x
    return np.tanh(y + f64(b))

@@ -1,0 +1,52 @@
+import concourse.mybir as mybir
+
+BF16 = mybir.dt.bfloat16
+F32 = mybir.dt.float32
+U16 = mybir.dt.uint16
+TANH = mybir.ActivationFunctionType.Tanh
+
+P = 128
+WORDS = 1024
+K = 256
+M = 128
+N = 1024
+K_BLOCKS = K // P
+PIECE = 512
+PIECES = N // PIECE
+OFFSETS_PER_COLUMN = 16
+
+FLOPS = 2 * K * M * N
+
+
+def tile_gather_matmul_kernel(tc, table, w, b, offs, out):
+    nc = tc.nc
+    with (
+        tc.tile_pool(name="held", bufs=1) as held,
+        tc.tile_pool(name="staging", bufs=PIECES) as staging,
+        tc.psum_pool(name="psum", bufs=1) as psum,
+    ):
+        offsets = held.tile([P, N // OFFSETS_PER_COLUMN], U16, name="offsets")
+        nc.sync.dma_start(offsets[:], offs)
+        weights = held.tile([P, K_BLOCKS, M], BF16, name="weights")
+        nc.scalar.dma_start(weights[:], w.rearrange("(a p) m -> p a m", p=P))
+        windows = [held.tile([P, WORDS], BF16, name=f"window{a}") for a in range(K_BLOCKS)]
+        nc.sync.dma_start(windows[0][:], table[0:P, :])
+        nc.scalar.dma_start(windows[1][:], table[P : 2 * P, :])
+        bias = held.tile([P, 1], F32, name="bias")
+        nc.scalar.dma_start(bias[:], b)
+
+        columns = PIECE // OFFSETS_PER_COLUMN
+        for piece in range(PIECES):
+            bank = psum.tile([P, PIECE], F32, name=f"bank{piece}")
+            piece_offsets = offsets[:, piece * columns : (piece + 1) * columns]
+            for a in range(K_BLOCKS):
+                nc.tensor.matmul(
+                    bank[:],
+                    weights[:, a, :],
+                    windows[a][:].indirect(piece_offsets),
+                    start=(a == 0),
+                    stop=(a == K_BLOCKS - 1),
+                )
+            result = staging.tile([P, PIECE], F32, name="result")
+            nc.scalar.activation(result[:], bank[:], TANH, bias=bias[:, 0:1])
+            nc.sync.dma_start(out[:, piece * PIECE : (piece + 1) * PIECE], result[:])

@@ -11,8 +11,9 @@ K = 256
 M = 128
 N = 1024
 K_BLOCKS = K // P
-PIECE = 512
+PIECE = 256
 PIECES = N // PIECE
+WARM_UP_MATMULS = 16
 OFFSETS_PER_COLUMN = 16
 
 FLOPS = 2 * K * M * N
@@ -29,24 +30,32 @@ def tile_gather_matmul_kernel(tc, table, w, b, offs, out):
         nc.sync.dma_start(offsets[:], offs)
         weights = held.tile([P, K_BLOCKS, M], BF16, name="weights")
         nc.scalar.dma_start(weights[:], w.rearrange("(a p) m -> p a m", p=P))
-        windows = [held.tile([P, WORDS], BF16, name=f"window{a}") for a in range(K_BLOCKS)]
-        nc.sync.dma_start(windows[0][:], table[0:P, :])
-        nc.scalar.dma_start(windows[1][:], table[P : 2 * P, :])
         bias = held.tile([P, 1], F32, name="bias")
-        nc.scalar.dma_start(bias[:], b)
+        nc.gpsimd.dma_start(bias[:], b)
+        windows = [held.tile([P, WORDS], BF16, name=f"window{a}") for a in range(K_BLOCKS)]
+        for a in range(K_BLOCKS):
+            nc.sync.dma_start(windows[a][:], table[a * P : (a + 1) * P, :])
+
+        zeros = held.tile([P, P], BF16, name="zeros")
+        nc.vector.memset(zeros[:], 0.0)
+        unused = psum.tile([P, P], F32, name="unused")
+        for turn in range(WARM_UP_MATMULS):
+            nc.tensor.matmul(unused[:], zeros[:], zeros[:], start=True, stop=True)
+        table_loaded = held.tile([P, 1], F32, name="table_loaded")
+        nc.scalar.activation(table_loaded[:], zeros[:, 0:1], TANH)
 
         columns = PIECE // OFFSETS_PER_COLUMN
-        for piece in range(PIECES):
-            bank = psum.tile([P, PIECE], F32, name=f"bank{piece}")
-            piece_offsets = offsets[:, piece * columns : (piece + 1) * columns]
-            for a in range(K_BLOCKS):
+        banks = [psum.tile([P, PIECE], F32, name=f"bank{piece}") for piece in range(PIECES)]
+        for a in range(K_BLOCKS):
+            for piece in range(PIECES):
                 nc.tensor.matmul(
-                    bank[:],
+                    banks[piece][:],
                     weights[:, a, :],
-                    windows[a][:].indirect(piece_offsets),
+                    windows[a][:].indirect(offsets[:, piece * columns : (piece + 1) * columns]),
                     start=(a == 0),
                     stop=(a == K_BLOCKS - 1),
                 )
+        for piece in range(PIECES):
             result = staging.tile([P, PIECE], F32, name="result")
-            nc.scalar.activation(result[:], bank[:], TANH, bias=bias[:, 0:1])
+            nc.scalar.activation(result[:], banks[piece][:], TANH, bias=bias[:, 0:1])
             nc.sync.dma_start(out[:, piece * PIECE : (piece + 1) * PIECE], result[:])

@@ -13,7 +13,6 @@ N = 1024
 K_BLOCKS = K // P
 PIECE = 256
 PIECES = N // PIECE
-WARM_UP_MATMULS = 16
 OFFSETS_PER_COLUMN = 16
 
 FLOPS = 2 * K * M * N
@@ -36,13 +35,10 @@ def tile_gather_matmul_kernel(tc, table, w, b, offs, out):
         for a in range(K_BLOCKS):
             nc.sync.dma_start(windows[a][:], table[a * P : (a + 1) * P, :])
 
-        zeros = held.tile([P, P], BF16, name="zeros")
+        zeros = held.tile([P, 1], F32, name="zeros")
         nc.vector.memset(zeros[:], 0.0)
-        unused = psum.tile([P, P], F32, name="unused")
-        for turn in range(WARM_UP_MATMULS):
-            nc.tensor.matmul(unused[:], zeros[:], zeros[:], start=True, stop=True)
         table_loaded = held.tile([P, 1], F32, name="table_loaded")
-        nc.scalar.activation(table_loaded[:], zeros[:, 0:1], TANH)
+        nc.scalar.activation(table_loaded[:], zeros[:], TANH)
 
         columns = PIECE // OFFSETS_PER_COLUMN
         banks = [psum.tile([P, PIECE], F32, name=f"bank{piece}") for piece in range(PIECES)]

@@ -30,7 +30,7 @@ def tile_gather_matmul_kernel(tc, table, w, b, offs, out):
         weights = held.tile([P, K_BLOCKS, M], BF16, name="weights")
         nc.scalar.dma_start(weights[:], w.rearrange("(a p) m -> p a m", p=P))
         bias = held.tile([P, 1], F32, name="bias")
-        nc.gpsimd.dma_start(bias[:], b)
+        nc.scalar.dma_start(bias[:], b)
         windows = [held.tile([P, WORDS], BF16, name=f"window{a}") for a in range(K_BLOCKS)]
         for a in range(K_BLOCKS):
             nc.sync.dma_start(windows[a][:], table[a * P : (a + 1) * P, :])

@@ -29,11 +29,11 @@ def tile_gather_matmul_kernel(tc, table, w, b, offs, out):
         nc.sync.dma_start(offsets[:], offs)
         weights = held.tile([P, K_BLOCKS, M], BF16, name="weights")
         nc.scalar.dma_start(weights[:], w.rearrange("(a p) m -> p a m", p=P))
+        windows = [held.tile([P, WORDS], BF16, name=f"window{a}") for a in range(K_BLOCKS)]
+        nc.sync.dma_start(windows[0][:], table[0:P, :])
+        nc.scalar.dma_start(windows[1][:], table[P : 2 * P, :])
         bias = held.tile([P, 1], F32, name="bias")
         nc.scalar.dma_start(bias[:], b)
-        windows = [held.tile([P, WORDS], BF16, name=f"window{a}") for a in range(K_BLOCKS)]
-        for a in range(K_BLOCKS):
-            nc.sync.dma_start(windows[a][:], table[a * P : (a + 1) * P, :])
 
         zeros = held.tile([P, 1], F32, name="zeros")
         nc.vector.memset(zeros[:], 0.0)
@@ -41,17 +41,17 @@ def tile_gather_matmul_kernel(tc, table, w, b, offs, out):
         nc.scalar.activation(table_loaded[:], zeros[:], TANH)
 
         columns = PIECE // OFFSETS_PER_COLUMN
-        banks = [psum.tile([P, PIECE], F32, name=f"bank{piece}") for piece in range(PIECES)]
-        for a in range(K_BLOCKS):
-            for piece in range(PIECES):
+        for piece in range(PIECES):
+            bank = psum.tile([P, PIECE], F32, name=f"bank{piece}")
+            piece_offsets = offsets[:, piece * columns : (piece + 1) * columns]
+            for a in range(K_BLOCKS):
                 nc.tensor.matmul(
-                    banks[piece][:],
+                    bank[:],
                     weights[:, a, :],
-                    windows[a][:].indirect(offsets[:, piece * columns : (piece + 1) * columns]),
+                    windows[a][:].indirect(piece_offsets),
                     start=(a == 0),
                     stop=(a == K_BLOCKS - 1),
                 )
-        for piece in range(PIECES):
             result = staging.tile([P, PIECE], F32, name="result")
-            nc.scalar.activation(result[:], banks[piece][:], TANH, bias=bias[:, 0:1])
+            nc.scalar.activation(result[:], bank[:], TANH, bias=bias[:, 0:1])
             nc.sync.dma_start(out[:, piece * PIECE : (piece + 1) * PIECE], result[:])

@@ -11,9 +11,9 @@ K = 256
 M = 128
 N = 1024
 K_BLOCKS = K // P
-PIECE = 256
-PIECES = N // PIECE
 OFFSETS_PER_COLUMN = 16
+PIECE_SIZES = (512, 256, 128, 128)
+assert sum(PIECE_SIZES) == N
 
 FLOPS = 2 * K * M * N
 
@@ -22,7 +22,7 @@ def tile_gather_matmul_kernel(tc, table, w, b, offs, out):
     nc = tc.nc
     with (
         tc.tile_pool(name="held", bufs=1) as held,
-        tc.tile_pool(name="staging", bufs=PIECES) as staging,
+        tc.tile_pool(name="staging", bufs=1) as staging,
         tc.psum_pool(name="psum", bufs=1) as psum,
     ):
         offsets = held.tile([P, N // OFFSETS_PER_COLUMN], U16, name="offsets")
@@ -40,10 +40,10 @@ def tile_gather_matmul_kernel(tc, table, w, b, offs, out):
         table_loaded = held.tile([P, 1], F32, name="table_loaded")
         nc.scalar.activation(table_loaded[:], zeros[:], TANH)
 
-        columns = PIECE // OFFSETS_PER_COLUMN
-        for piece in range(PIECES):
-            bank = psum.tile([P, PIECE], F32, name=f"bank{piece}")
-            piece_offsets = offsets[:, piece * columns : (piece + 1) * columns]
+        first = 0
+        for piece, size in enumerate(PIECE_SIZES):
+            bank = psum.tile([P, size], F32, name=f"bank{piece}")
+            piece_offsets = offsets[:, first // OFFSETS_PER_COLUMN : (first + size) // OFFSETS_PER_COLUMN]
             for a in range(K_BLOCKS):
                 nc.tensor.matmul(
                     bank[:],
@@ -52,6 +52,7 @@ def tile_gather_matmul_kernel(tc, table, w, b, offs, out):
                     start=(a == 0),
                     stop=(a == K_BLOCKS - 1),
                 )
-            result = staging.tile([P, PIECE], F32, name="result")
+            result = staging.tile([P, size], F32, name=f"result{piece}")
             nc.scalar.activation(result[:], bank[:], TANH, bias=bias[:, 0:1])
-            nc.sync.dma_start(out[:, piece * PIECE : (piece + 1) * PIECE], result[:])
+            nc.sync.dma_start(out[:, first : first + size], result[:])
+            first += size

@@ -12,7 +12,7 @@ M = 128
 N = 1024
 K_BLOCKS = K // P
 OFFSETS_PER_COLUMN = 16
-PIECE_SIZES = (512, 256, 128, 128)
+PIECE_SIZES = (384, 384, 256)
 assert sum(PIECE_SIZES) == N
 
 FLOPS = 2 * K * M * N

@@ -12,7 +12,7 @@ M = 128
 N = 1024
 K_BLOCKS = K // P
 OFFSETS_PER_COLUMN = 16
-PIECE_SIZES = (384, 384, 256)
+PIECE_SIZES = (448, 320, 256)
 assert sum(PIECE_SIZES) == N
 
 FLOPS = 2 * K * M * N

@@ -12,7 +12,7 @@ M = 128
 N = 1024
 K_BLOCKS = K // P
 OFFSETS_PER_COLUMN = 16
-PIECE_SIZES = (448, 320, 256)
+PIECE_SIZES = (480, 320, 224)
 assert sum(PIECE_SIZES) == N
 
 FLOPS = 2 * K * M * N
@@ -54,5 +54,6 @@ def tile_gather_matmul_kernel(tc, table, w, b, offs, out):
                 )
             result = staging.tile([P, size], F32, name=f"result{piece}")
             nc.scalar.activation(result[:], bank[:], TANH, bias=bias[:, 0:1])
-            nc.sync.dma_start(out[:, first : first + size], result[:])
+            store_queue = nc.scalar if first + size == N else nc.sync
+            store_queue.dma_start(out[:, first : first + size], result[:])
             first += size

import concourse.mybir as mybir

BF16 = mybir.dt.bfloat16
F32 = mybir.dt.float32
U16 = mybir.dt.uint16
TANH = mybir.ActivationFunctionType.Tanh

P = 128
WORDS = 1024
K = 256
M = 128
N = 1024
K_BLOCKS = K // P
OFFSETS_PER_COLUMN = 16
PIECE_SIZES = (480, 320, 224)
assert sum(PIECE_SIZES) == N

FLOPS = 2 * K * M * N


def tile_gather_matmul_kernel(tc, table, w, b, offs, out):
    nc = tc.nc
    with (
        tc.tile_pool(name="held", bufs=1) as held,
        tc.tile_pool(name="staging", bufs=1) as staging,
        tc.psum_pool(name="psum", bufs=1) as psum,
    ):
        offsets = held.tile([P, N // OFFSETS_PER_COLUMN], U16, name="offsets")
        nc.sync.dma_start(offsets[:], offs)
        weights = held.tile([P, K_BLOCKS, M], BF16, name="weights")
        nc.scalar.dma_start(weights[:], w.rearrange("(a p) m -> p a m", p=P))
        windows = [held.tile([P, WORDS], BF16, name=f"window{a}") for a in range(K_BLOCKS)]
        nc.sync.dma_start(windows[0][:], table[0:P, :])
        nc.scalar.dma_start(windows[1][:], table[P : 2 * P, :])
        bias = held.tile([P, 1], F32, name="bias")
        nc.scalar.dma_start(bias[:], b)

        zeros = held.tile([P, 1], F32, name="zeros")
        nc.vector.memset(zeros[:], 0.0)
        table_loaded = held.tile([P, 1], F32, name="table_loaded")
        nc.scalar.activation(table_loaded[:], zeros[:], TANH)

        first = 0
        for piece, size in enumerate(PIECE_SIZES):
            bank = psum.tile([P, size], F32, name=f"bank{piece}")
            piece_offsets = offsets[:, first // OFFSETS_PER_COLUMN : (first + size) // OFFSETS_PER_COLUMN]
            for a in range(K_BLOCKS):
                nc.tensor.matmul(
                    bank[:],
                    weights[:, a, :],
                    windows[a][:].indirect(piece_offsets),
                    start=(a == 0),
                    stop=(a == K_BLOCKS - 1),
                )
            result = staging.tile([P, size], F32, name=f"result{piece}")
            nc.scalar.activation(result[:], bank[:], TANH, bias=bias[:, 0:1])
            store_queue = nc.scalar if first + size == N else nc.sync
            store_queue.dma_start(out[:, first : first + size], result[:])
            first += size
